import numpy as np
import ml_dtypes


def mxq(x, axis, fmt="e4m3"):
    dtype, down = {"e4m3": (ml_dtypes.float8_e4m3fn, 7), "e5m2": (ml_dtypes.float8_e5m2, 14)}[fmt]
    v = np.moveaxis(np.asarray(x, np.float32).astype(ml_dtypes.bfloat16).astype(np.float64), axis, -1)
    blocks = v.reshape(v.shape[:-1] + (-1, 32))
    amax = np.abs(blocks).max(-1, keepdims=True)
    byte = np.maximum(np.where(amax > 0, np.frexp(amax)[1] - 1 + 127, 0) - down, 1)
    scale = np.exp2(byte - 127.0)
    codes = (blocks / scale).astype(np.float32).astype(dtype).astype(np.float64)
    return np.moveaxis((codes * scale).reshape(v.shape), -1, axis)


WIDE = False


def mx_kscale(k):
    if not WIDE:
        return np.ones(k)
    levels = np.array([10, -10, 5, -5, 0])
    if k % 512:
        return np.exp2(np.random.permutation(np.resize(levels, k // 32))).repeat(32)
    a = np.empty((k // 512, 16))
    for p in range(k // 512):
        a[p, :8] = np.random.permutation(np.resize(levels, 8))
        for g in range(8):
            far = levels[np.abs(levels - a[p, g]) >= 10]
            a[p, g + 8] = far[np.random.randint(len(far))]
    return np.exp2(a.ravel()).repeat(32)


def f64(x):
    return np.asarray(x).astype(np.float64)


def striped(idx):
    return np.tile(idx.reshape(-1, 16).T, (8, 1)).astype(np.uint16)


def unstriped(offs):
    return offs[:16].T.reshape(-1).astype(np.int64)


E2M1 = np.array([0.0, 0.5, 1.0, 1.5, 2.0, 3.0, 4.0, 6.0, -0.0, -0.5, -1.0, -1.5, -2.0, -3.0, -4.0, -6.0])


def pack_weight(w, fmt):
    k, n = w.shape
    w = f64(np.asarray(w, np.float32).astype(ml_dtypes.bfloat16)).reshape(k // 32, 32, n)
    amax = np.abs(w).max(1)
    if fmt == "e4m3":
        byte = np.frexp(amax)[1] - 1 + 127 - 7
    else:
        mant, ex = np.frexp(amax / 6.0)
        byte = np.where(mant > 0.5, ex, ex - 1) + 127
    byte = np.clip(np.where(amax > 0, byte, 1), 1, 254)
    scaled = (w * np.exp2(127.0 - byte)[:, None, :]).reshape(k, n).astype(np.float32)
    by_word = np.ascontiguousarray(scaled.reshape(k // 512, 128, 4, n).transpose(0, 1, 3, 2))
    if fmt == "e4m3":
        words = by_word.astype(ml_dtypes.float8_e4m3fn).view(np.uint8)
    else:
        c = by_word.astype(ml_dtypes.float4_e2m1fn).view(np.uint8) & 0xF
        words = (c[..., 0::2] | (c[..., 1::2] << 4)).reshape(k // 512, 128, 2 * n)
    return np.ascontiguousarray(words), np.ascontiguousarray(byte.astype(np.uint8).reshape(k // 512, 16, n))


def unpack_weight(words, scales, fmt):
    g, _, n = scales.shape
    words = np.ascontiguousarray(words).reshape(g, 128, n, -1)
    if fmt == "e4m3":
        vals = words.view(ml_dtypes.float8_e4m3fn).astype(np.float64)
    else:
        nib = np.empty((g, 128, n, 4), np.uint8)
        nib[..., 0::2] = words & 0xF
        nib[..., 1::2] = words >> 4
        vals = E2M1[nib]
    vals = vals * np.repeat(np.exp2(scales.astype(np.float64) - 127.0), 8, axis=1)[..., None]
    return vals.transpose(0, 1, 3, 2).reshape(g * 512, n)


K, T, E, C, N = 1024, 640, 10, 128, 384


def by_expert(wq, xq):
    return np.concatenate([wq[e].T @ xq[:, e * C:(e + 1) * C] for e in range(E)], axis=1)


def setup_inputs():
    n = np.random.standard_normal
    s = mx_kscale(K)[:, None]
    first = np.random.permutation(np.repeat(np.arange(E), T // E))
    second = (first + 1 + np.random.permutation(np.repeat(np.arange(E - 1), -(-T // (E - 1)))[:T])) % E
    while np.bincount(second, minlength=E).max() != T // E:
        load = np.bincount(second, minlength=E); hi, lo = int(load.argmax()), int(load.argmin())
        t = np.flatnonzero((second == hi) & (first != lo))[0]; second[t] = lo
    slot_token = np.empty(E * C, np.int64); pos = np.empty((2, T), np.int64); fill = np.zeros(E, np.int64)
    place = np.stack([np.random.permutation(C) for _ in range(E)])
    for r, deal in enumerate((first, second)):
        for t in np.random.permutation(T):
            e = deal[t]; j = e * C + place[e, fill[e]]; fill[e] += 1; slot_token[j] = t; pos[r, t] = j
    g = np.random.uniform(0.2, 0.8, T)
    w = [pack_weight(m, "e2m1") for m in n((E + 1, K, N)) / np.sqrt(K) / s[None]]
    return {
        "xT": (n((K, T)) * s).astype(np.float32),
        "w_words": np.stack([m[0] for m in w]),
        "w_scales": np.stack([m[1] for m in w]),
        "gate": np.stack([np.tile(g, (N, 1)), np.tile(1.0 - g, (N, 1))]).astype(np.float32),
        "offs": striped(slot_token),
        "pos1": striped(pos[0]),
        "pos2": striped(pos[1]),
    }


def reference(xT, w_words, w_scales, gate, offs, pos1, pos2):
    idx = unstriped(offs)
    w = np.stack([unpack_weight(w_words[e], w_scales[e], "e2m1") for e in range(E + 1)])
    wq = w
    xs = mxq(f64(xT), 0, "e4m3")
    ys = wq[E].T @ xs
    xq = mxq(f64(xT)[:, idx], 0, "e4m3")
    y = by_expert(w, xq)
    return ys + f64(gate[0]) * y[:, unstriped(pos1)] + f64(gate[1]) * y[:, unstriped(pos2)]

@@ -1,0 +1,179 @@
+from contextlib import ExitStack
+
+import concourse.mybir as mybir
+
+K, T, E, C, N = 1024, 640, 10, 128, 384
+S = E * C
+FLOPS = 2 * K * N * (S + T)
+
+F32 = mybir.dt.float32
+BF16 = mybir.dt.bfloat16
+U32 = mybir.dt.uint32
+I32 = mybir.dt.int32
+U16 = mybir.dt.uint16
+U8 = mybir.dt.uint8
+FP8X4 = mybir.dt.float8_e4m3fn_x4
+FP4X4 = mybir.dt.float4_e2m1fn_x4
+MULT = mybir.AluOpType.mult
+ADD = mybir.AluOpType.add
+
+P = 128
+PASSES = 2
+M = N // P
+
+
+def tile_moe_shr_lin_none_kernel(tc, xT, w_words, w_scales, gate, offs, pos1, pos2, out):
+    nc = tc.nc
+    with ExitStack() as ctx:
+        keep = ctx.enter_context(tc.tile_pool(name="keep", bufs=1))
+        work = ctx.enter_context(tc.tile_pool(name="work", bufs=1))
+        psum = ctx.enter_context(tc.psum_pool(name="psum", bufs=1))
+
+        offs_t = keep.tile([P, S // 16], U16, name="offs_t")
+        pos1_t = keep.tile([P, T // 16], U16, name="pos1_t")
+        pos2_t = keep.tile([P, T // 16], U16, name="pos2_t")
+
+        raw = {}
+        for a in range(PASSES):
+            for u in range(2):
+                raw[a, u] = work.tile([P, 2, T], F32, name=f"raw{a}{u}")
+        x_view = xT.rearrange("(a p u j) t -> a u p j t", a=PASSES, p=P, u=2, j=2)
+        nc.sync.dma_start(raw[0, 0][:], x_view[0, 0])
+        nc.sync.dma_start(offs_t[:], offs)
+        nc.sync.dma_start(raw[0, 1][:], x_view[0, 1])
+        nc.sync.dma_start(raw[1, 0][:], x_view[1, 0])
+        nc.sync.dma_start(raw[1, 1][:], x_view[1, 1])
+
+        ws = work.tile([P, (E + 1) * PASSES, N], U8, name="ws", align_bytes=64)
+        nc.vector.memset(ws[:].rearrange("p e n -> p (e n)").bitcast(I32), 0)
+        s_view = w_scales.rearrange("e a q n -> q (e a) n").bitcast(I32)
+        for q in range(4):
+            nc.sync.dma_start(ws[32 * q : 32 * q + 4].bitcast(I32), s_view[4 * q : 4 * q + 4])
+
+        ww = work.tile([P, (E + 1) * PASSES, 2 * N], U8, name="ww", align_bytes=64)
+        w_view = w_words.rearrange("e a p b -> p (e a) b").bitcast(I32)
+        for e0, e1 in ((0, 4), (4, 8), (8, 11)):
+            nc.sync.dma_start(ww[:, PASSES * e0 : PASSES * e1, :].bitcast(I32), w_view[:, PASSES * e0 : PASSES * e1, :])
+        nc.sync.dma_start(pos1_t[:], pos1)
+        nc.sync.dma_start(pos2_t[:], pos2)
+        gates = []
+        for m in range(M):
+            g = work.tile([P, 2, T], F32, name=f"gate{m}")
+            nc.sync.dma_start(g[:], gate[:, m * P : (m + 1) * P, :].rearrange("g p t -> p g t"))
+            gates.append(g)
+
+        pairs = [work.tile([P, 2, T, 2], BF16, name=f"pairs{a}", align_bytes=64) for a in range(PASSES)]
+        slots = [work.tile([P, S, 4], BF16, name=f"slots{a}", align_bytes=64) for a in range(PASSES)]
+        slot_codes = [work.tile([P, S], U32, name=f"slot_codes{a}", align_bytes=64) for a in range(PASSES)]
+        slot_scales = [work.tile([P, S], U8, name=f"slot_scales{a}", align_bytes=64) for a in range(PASSES)]
+        toks = work.tile([P, PASSES * T, 4], BF16, name="toks", align_bytes=64)
+        tok_codes = work.tile([P, PASSES * T], U32, name="tok_codes", align_bytes=64)
+        tok_scales = work.tile([P, PASSES * T], U8, name="tok_scales", align_bytes=64)
+
+        def cast(engine_copy, a, u, t0, t1):
+            engine_copy(out=pairs[a][:, u, t0:t1, :], in_=raw[a, u][:, :, t0:t1].rearrange("p j t -> p t j"))
+
+        def gather(a, u, lo, hi):
+            window = pairs[a][:, u, :, :].rearrange("p t d -> p (t d)").bitcast(U32)
+            dst = slots[a][:].rearrange("p s d -> p (s d)").bitcast(U32).rearrange("p (s u) -> p s u", u=2)
+            nc.vector.tensor_copy(dst[:, lo:hi, u], window.indirect(offs_t[:, lo // 16 : hi // 16]))
+
+        def quantize_slots(a, lo, hi):
+            nc.vector.quantize_mx(
+                out=slot_codes[a][:, lo:hi].bitcast(FP8X4),
+                scales=slot_scales[a][:, lo:hi],
+                in_=slots[a][:, lo:hi, :].rearrange("p s d -> p (s d)"),
+            )
+
+        def quantize_toks(lo, hi):
+            nc.vector.quantize_mx(
+                out=tok_codes[:, lo:hi].bitcast(FP8X4),
+                scales=tok_scales[:, lo:hi],
+                in_=toks[:, lo:hi, :].rearrange("p s d -> p (s d)"),
+            )
+
+        def interleave_toks(a):
+            src = pairs[a][:].rearrange("p u t d -> p (u t d)").bitcast(U32).rearrange("p (u t) -> p t u", u=2)
+            dst = toks[:, a * T : (a + 1) * T, :].rearrange("p t d -> p (t d)").bitcast(U32).rearrange("p (t u) -> p t u", u=2)
+            nc.scalar.copy(out=dst, in_=src)
+
+        def matmul(dst, e, a, m, codes, scales):
+            nc.tensor.matmul_mx(
+                out=dst,
+                lhsT=ww[:, PASSES * e + a, 2 * m * P : 2 * (m + 1) * P].bitcast(FP4X4),
+                lhsT_scale=ws[:, PASSES * e + a, m * P : (m + 1) * P],
+                rhs=codes.bitcast(FP8X4),
+                rhs_scale=scales,
+                start=(a == 0),
+                stop=(a == PASSES - 1),
+            )
+
+        y = [work.tile([P, S], F32, name=f"y{m}") for m in range(M)]
+
+        def experts(e0, e1):
+            for m in range(M):
+                bank = psum.tile([P, 512], F32, name="bank", bufs=4)
+                for e in range(e0, e1):
+                    for a in range(PASSES):
+                        cols = slice(e * C, (e + 1) * C)
+                        matmul(bank[:, (e - e0) * C : (e - e0 + 1) * C], e, a, m, slot_codes[a][:, cols], slot_scales[a][:, cols])
+                nc.scalar.copy(out=y[m][:, e0 * C : e1 * C], in_=bank[:, : (e1 - e0) * C])
+
+        cast(nc.vector.tensor_copy, 0, 0, 0, 432)
+        cast(nc.scalar.copy, 0, 0, 432, T)
+        cast(nc.scalar.copy, 0, 1, 0, T)
+        cast(nc.scalar.copy, 1, 0, 0, T)
+        cast(nc.scalar.copy, 1, 1, 0, T)
+        for u in range(2):
+            for lo, hi in ((0, 448), (448, 864), (864, S)):
+                gather(0, u, lo, hi)
+        for a in range(PASSES):
+            interleave_toks(a)
+
+        def gather_late(lo, hi):
+            for u in range(2):
+                for l in range(lo, hi, 256):
+                    gather(1, u, l, min(hi, l + 256))
+
+        gather_late(0, 512)
+        quantize_slots(0, 0, 1024)
+        quantize_slots(0, 1024, S)
+        quantize_slots(1, 0, 512)
+        experts(0, 4)
+        gather_late(512, 1024)
+        quantize_toks(0, 1024)
+        quantize_slots(1, 512, 1024)
+        experts(4, 8)
+        gather_late(1024, S)
+        quantize_toks(1024, PASSES * T)
+        quantize_slots(1, 1024, S)
+        experts(8, 10)
+
+        ys = [psum.tile([P, 512], F32, name=f"ys{m}") for m in range(M)]
+        ys_tail = psum.tile([P, M, P], F32, name="ys_tail")
+        for m in range(M):
+            for dst, lo, hi in ((ys[m][:], 0, 512), (ys_tail[:, m, :], 512, T)):
+                for a in range(PASSES):
+                    matmul(dst, E, a, m, tok_codes[:, a * T + lo : a * T + hi], tok_scales[:, a * T + lo : a * T + hi])
+
+        first = [work.tile([P, T], F32, name=f"first{m}") for m in range(M)]
+        second = [work.tile([P, T], F32, name=f"second{m}") for m in range(M)]
+        both = [work.tile([P, T], F32, name=f"both{m}") for m in range(M)]
+        res = [work.tile([P, T], F32, name=f"res{m}") for m in range(M)]
+
+        def pick(m):
+            nc.vector.tensor_tensor(first[m][:], y[m][:].indirect(pos1_t[:]), gates[m][:, 0, :], MULT)
+            nc.vector.tensor_tensor(second[m][:], y[m][:].indirect(pos2_t[:]), gates[m][:, 1, :], MULT)
+
+        def finish(m):
+            nc.vector.tensor_tensor(both[m][:], first[m][:], second[m][:], ADD)
+            for src, lo, hi in ((ys[m][:], 0, 512), (ys_tail[:, m, :], 512, T)):
+                nc.vector.tensor_tensor(res[m][:, lo:hi], src, both[m][:, lo:hi], ADD)
+                nc.sync.dma_start(out[m * P : (m + 1) * P, lo:hi], res[m][:, lo:hi])
+
+        pick(0)
+        pick(1)
+        finish(0)
+        pick(2)
+        finish(1)
+        finish(2)

@@ -63,6 +63,7 @@ def tile_moe_shr_lin_none_kernel(tc, xT, w_words, w_scales, gate, offs, pos1, po
             gates.append(g)
 
         pairs = [work.tile([P, 2, T, 2], BF16, name=f"pairs{a}", align_bytes=64) for a in range(PASSES)]
+        planes = [work.tile([P, 2, S, 2], BF16, name=f"planes{a}", align_bytes=64) for a in range(PASSES)]
         slots = [work.tile([P, S, 4], BF16, name=f"slots{a}", align_bytes=64) for a in range(PASSES)]
         slot_codes = [work.tile([P, S], U32, name=f"slot_codes{a}", align_bytes=64) for a in range(PASSES)]
         slot_scales = [work.tile([P, S], U8, name=f"slot_scales{a}", align_bytes=64) for a in range(PASSES)]
@@ -75,8 +76,13 @@ def tile_moe_shr_lin_none_kernel(tc, xT, w_words, w_scales, gate, offs, pos1, po
 
         def gather(a, u, lo, hi):
             window = pairs[a][:, u, :, :].rearrange("p t d -> p (t d)").bitcast(U32)
-            dst = slots[a][:].rearrange("p s d -> p (s d)").bitcast(U32).rearrange("p (s u) -> p s u", u=2)
-            nc.vector.tensor_copy(dst[:, lo:hi, u], window.indirect(offs_t[:, lo // 16 : hi // 16]))
+            dst = planes[a][:, u, lo:hi, :].rearrange("p s d -> p (s d)").bitcast(U32)
+            nc.vector.tensor_copy(dst, window.indirect(offs_t[:, lo // 16 : hi // 16]))
+
+        def interleave_slots(copy, dtype, a, lo, hi):
+            src = planes[a][:].rearrange("p u s d -> p (u s d)").bitcast(dtype).rearrange("p (u s) -> p s u", u=2)
+            dst = slots[a][:].rearrange("p s d -> p (s d)").bitcast(dtype).rearrange("p (s u) -> p s u", u=2)
+            copy(out=dst[:, lo:hi, :], in_=src[:, lo:hi, :])
 
         def quantize_slots(a, lo, hi):
             nc.vector.quantize_mx(
@@ -127,8 +133,9 @@ def tile_moe_shr_lin_none_kernel(tc, xT, w_words, w_scales, gate, offs, pos1, po
         for u in range(2):
             for lo, hi in ((0, 448), (448, 864), (864, S)):
                 gather(0, u, lo, hi)
-        for a in range(PASSES):
-            interleave_toks(a)
+        interleave_slots(nc.scalar.copy, U32, 0, 0, 1024)
+        interleave_slots(nc.scalar.copy, U32, 0, 1024, S)
+        interleave_toks(0)
 
         def gather_late(lo, hi):
             for u in range(2):
@@ -136,18 +143,22 @@ def tile_moe_shr_lin_none_kernel(tc, xT, w_words, w_scales, gate, offs, pos1, po
                     gather(1, u, l, min(hi, l + 256))
 
         gather_late(0, 512)
+        interleave_slots(nc.scalar.copy, U32, 1, 0, 512)
         quantize_slots(0, 0, 1024)
         quantize_slots(0, 1024, S)
+        interleave_toks(1)
+        gather_late(512, 1024)
+        interleave_slots(nc.scalar.copy, U32, 1, 512, 1024)
         quantize_slots(1, 0, 512)
         experts(0, 4)
-        gather_late(512, 1024)
-        quantize_toks(0, 1024)
+        gather_late(1024, S)
         quantize_slots(1, 512, 1024)
         experts(4, 8)
-        gather_late(1024, S)
-        quantize_toks(1024, PASSES * T)
+        interleave_slots(nc.vector.tensor_copy, I32, 1, 1024, S)
+        quantize_toks(0, 1024)
         quantize_slots(1, 1024, S)
         experts(8, 10)
+        quantize_toks(1024, PASSES * T)
 
         ys = [psum.tile([P, 512], F32, name=f"ys{m}") for m in range(M)]
         ys_tail = psum.tile([P, M, P], F32, name="ys_tail")

@@ -38,7 +38,8 @@ def tile_moe_shr_lin_none_kernel(tc, xT, w_words, w_scales, gate, offs, pos1, po
             for u in range(2):
                 raw[a, u] = work.tile([P, 2, T], F32, name=f"raw{a}{u}")
         x_view = xT.rearrange("(a p u j) t -> a u p j t", a=PASSES, p=P, u=2, j=2)
-        nc.sync.dma_start(raw[0, 0][:], x_view[0, 0])
+        nc.sync.dma_start(raw[0, 0][:, :, :320], x_view[0, 0][:, :, :320])
+        nc.sync.dma_start(raw[0, 0][:, :, 320:], x_view[0, 0][:, :, 320:])
         nc.sync.dma_start(offs_t[:], offs)
         nc.sync.dma_start(raw[0, 1][:], x_view[0, 1])
         nc.sync.dma_start(raw[1, 0][:], x_view[1, 0])
@@ -62,7 +63,9 @@ def tile_moe_shr_lin_none_kernel(tc, xT, w_words, w_scales, gate, offs, pos1, po
             nc.sync.dma_start(g[:], gate[:, m * P : (m + 1) * P, :].rearrange("g p t -> p g t"))
             gates.append(g)
 
-        pairs = [work.tile([P, 2, T, 2], BF16, name=f"pairs{a}", align_bytes=64) for a in range(PASSES)]
+        pairs = work.tile([P, 2 * PASSES, T, 2], BF16, name="pairs", align_bytes=64)
+        pair_words = pairs[:].rearrange("p b t d -> p (b t d)").bitcast(U32)
+        block = {(1, 0): 0, (1, 1): 1, (0, 0): 2, (0, 1): 3}
         planes = [work.tile([P, 2, S, 2], BF16, name=f"planes{a}", align_bytes=64) for a in range(PASSES)]
         slots = [work.tile([P, S, 4], BF16, name=f"slots{a}", align_bytes=64) for a in range(PASSES)]
         slot_codes = [work.tile([P, S], U32, name=f"slot_codes{a}", align_bytes=64) for a in range(PASSES)]
@@ -72,10 +75,12 @@ def tile_moe_shr_lin_none_kernel(tc, xT, w_words, w_scales, gate, offs, pos1, po
         tok_scales = work.tile([P, PASSES * T], U8, name="tok_scales", align_bytes=64)
 
         def cast(engine_copy, a, u, t0, t1):
-            engine_copy(out=pairs[a][:, u, t0:t1, :], in_=raw[a, u][:, :, t0:t1].rearrange("p j t -> p t j"))
+            engine_copy(out=pairs[:, block[a, u], t0:t1, :], in_=raw[a, u][:, :, t0:t1].rearrange("p j t -> p t j"))
 
         def gather(a, u, lo, hi):
-            window = pairs[a][:, u, :, :].rearrange("p t d -> p (t d)").bitcast(U32)
+            start = block[a, u] * T
+            stop = start + T if a == 0 else start + 2 * T
+            window = pair_words[:, start:stop]
             dst = planes[a][:, u, lo:hi, :].rearrange("p s d -> p (s d)").bitcast(U32)
             nc.vector.tensor_copy(dst, window.indirect(offs_t[:, lo // 16 : hi // 16]))
 
@@ -99,7 +104,7 @@ def tile_moe_shr_lin_none_kernel(tc, xT, w_words, w_scales, gate, offs, pos1, po
             )
 
         def interleave_toks(a):
-            src = pairs[a][:].rearrange("p u t d -> p (u t d)").bitcast(U32).rearrange("p (u t) -> p t u", u=2)
+            src = pair_words[:, block[a, 0] * T : (block[a, 0] + 2) * T].rearrange("p (u t) -> p t u", u=2)
             dst = toks[:, a * T : (a + 1) * T, :].rearrange("p t d -> p (t d)").bitcast(U32).rearrange("p (t u) -> p t u", u=2)
             nc.scalar.copy(out=dst, in_=src)
 
@@ -116,75 +121,90 @@ def tile_moe_shr_lin_none_kernel(tc, xT, w_words, w_scales, gate, offs, pos1, po
 
         y = [work.tile([P, S], F32, name=f"y{m}") for m in range(M)]
 
-        def experts(e0, e1):
-            for m in range(M):
-                bank = psum.tile([P, 512], F32, name="bank", bufs=4)
-                for e in range(e0, e1):
-                    for a in range(PASSES):
-                        cols = slice(e * C, (e + 1) * C)
-                        matmul(bank[:, (e - e0) * C : (e - e0 + 1) * C], e, a, m, slot_codes[a][:, cols], slot_scales[a][:, cols])
-                nc.scalar.copy(out=y[m][:, e0 * C : e1 * C], in_=bank[:, : (e1 - e0) * C])
+        def experts(m, e0, e1):
+            bank = psum.tile([P, 512], F32, name="bank", bufs=4)
+            for e in range(e0, e1):
+                for a in range(PASSES):
+                    cols = slice(e * C, (e + 1) * C)
+                    matmul(bank[:, (e - e0) * C : (e - e0 + 1) * C], e, a, m, slot_codes[a][:, cols], slot_scales[a][:, cols])
+            nc.scalar.copy(out=y[m][:, e0 * C : e1 * C], in_=bank[:, : (e1 - e0) * C])
 
-        cast(nc.vector.tensor_copy, 0, 0, 0, 432)
-        cast(nc.scalar.copy, 0, 0, 432, T)
+        for half in (0, 320):
+            cast(nc.vector.tensor_copy, 0, 0, half, half + 208)
+            cast(nc.scalar.copy, 0, 0, half + 208, half + 320)
         cast(nc.scalar.copy, 0, 1, 0, T)
         cast(nc.scalar.copy, 1, 0, 0, T)
         cast(nc.scalar.copy, 1, 1, 0, T)
+        for lo, hi in ((0, 448), (448, 864), (864, S)):
+            gather(0, 0, lo, hi)
+        for half in (0, 640):
+            gather(0, 1, half, half + 320)
+            gather(0, 1, half + 320, half + 640)
+            interleave_slots(nc.scalar.copy, U32, 0, half, half + 640)
         for u in range(2):
-            for lo, hi in ((0, 448), (448, 864), (864, S)):
-                gather(0, u, lo, hi)
-        interleave_slots(nc.scalar.copy, U32, 0, 0, 1024)
-        interleave_slots(nc.scalar.copy, U32, 0, 1024, S)
-        interleave_toks(0)
-
-        def gather_late(lo, hi):
-            for u in range(2):
-                for l in range(lo, hi, 256):
-                    gather(1, u, l, min(hi, l + 256))
-
-        gather_late(0, 512)
+            gather(1, u, 0, 512)
         interleave_slots(nc.scalar.copy, U32, 1, 0, 512)
         quantize_slots(0, 0, 1024)
         quantize_slots(0, 1024, S)
-        interleave_toks(1)
-        gather_late(512, 1024)
+        for u in range(2):
+            gather(1, u, 512, 1024)
         interleave_slots(nc.scalar.copy, U32, 1, 512, 1024)
         quantize_slots(1, 0, 512)
-        experts(0, 4)
-        gather_late(1024, S)
+        for m in range(M):
+            experts(m, 0, 4)
+        for u in range(2):
+            gather(1, u, 1024, S)
         quantize_slots(1, 512, 1024)
-        experts(4, 8)
         interleave_slots(nc.vector.tensor_copy, I32, 1, 1024, S)
-        quantize_toks(0, 1024)
+        interleave_toks(0)
+        interleave_toks(1)
         quantize_slots(1, 1024, S)
-        experts(8, 10)
+        for m in range(M):
+            experts(m, 4, 8)
+            experts(m, 8, 10)
+        quantize_toks(0, 1024)
         quantize_toks(1024, PASSES * T)
 
         ys = [psum.tile([P, 512], F32, name=f"ys{m}") for m in range(M)]
+        shared = [work.tile([P, T], F32, name=f"shared{m}") for m in range(M)]
         ys_tail = psum.tile([P, M, P], F32, name="ys_tail")
         for m in range(M):
             for dst, lo, hi in ((ys[m][:], 0, 512), (ys_tail[:, m, :], 512, T)):
                 for a in range(PASSES):
                     matmul(dst, E, a, m, tok_codes[:, a * T + lo : a * T + hi], tok_scales[:, a * T + lo : a * T + hi])
+            nc.scalar.copy(out=shared[m][:, :512], in_=ys[m][:])
+            nc.scalar.copy(out=shared[m][:, 512:], in_=ys_tail[:, m, :])
 
         first = [work.tile([P, T], F32, name=f"first{m}") for m in range(M)]
         second = [work.tile([P, T], F32, name=f"second{m}") for m in range(M)]
         both = [work.tile([P, T], F32, name=f"both{m}") for m in range(M)]
         res = [work.tile([P, T], F32, name=f"res{m}") for m in range(M)]
 
-        def pick(m):
+        def pick1(m):
             nc.vector.tensor_tensor(first[m][:], y[m][:].indirect(pos1_t[:]), gates[m][:, 0, :], MULT)
-            nc.vector.tensor_tensor(second[m][:], y[m][:].indirect(pos2_t[:]), gates[m][:, 1, :], MULT)
 
-        def finish(m):
-            nc.vector.tensor_tensor(both[m][:], first[m][:], second[m][:], ADD)
-            for src, lo, hi in ((ys[m][:], 0, 512), (ys_tail[:, m, :], 512, T)):
-                nc.vector.tensor_tensor(res[m][:, lo:hi], src, both[m][:, lo:hi], ADD)
-                nc.sync.dma_start(out[m * P : (m + 1) * P, lo:hi], res[m][:, lo:hi])
+        def pick2(m, lo, hi):
+            nc.vector.tensor_tensor(second[m][:, lo:hi], y[m][:].indirect(pos2_t[:, lo // 16 : hi // 16]), gates[m][:, 1, lo:hi], MULT)
 
-        pick(0)
-        pick(1)
-        finish(0)
-        pick(2)
-        finish(1)
-        finish(2)
+        def add(m, lo, hi):
+            nc.vector.tensor_tensor(both[m][:, lo:hi], first[m][:, lo:hi], second[m][:, lo:hi], ADD)
+
+        def finish(m, lo, hi):
+            nc.vector.tensor_tensor(res[m][:, lo:hi], shared[m][:, lo:hi], both[m][:, lo:hi], ADD)
+            nc.sync.dma_start(out[m * P : (m + 1) * P, lo:hi], res[m][:, lo:hi])
+
+        pick1(0)
+        pick2(0, 0, T)
+        pick1(1)
+        add(0, 0, T)
+        pick2(1, 0, T)
+        finish(0, 0, T)
+        pick1(2)
+        add(1, 0, T)
+        pick2(2, 0, 448)
+        finish(1, 0, T)
+        pick2(2, 448, T)
+        add(2, 0, 448)
+        add(2, 448, T)
+        finish(2, 0, 448)
+        finish(2, 448, T)

@@ -66,7 +66,6 @@ def tile_moe_shr_lin_none_kernel(tc, xT, w_words, w_scales, gate, offs, pos1, po
         pairs = work.tile([P, 2 * PASSES, T, 2], BF16, name="pairs", align_bytes=64)
         pair_words = pairs[:].rearrange("p b t d -> p (b t d)").bitcast(U32)
         block = {(1, 0): 0, (1, 1): 1, (0, 0): 2, (0, 1): 3}
-        planes = [work.tile([P, 2, S, 2], BF16, name=f"planes{a}", align_bytes=64) for a in range(PASSES)]
         slots = [work.tile([P, S, 4], BF16, name=f"slots{a}", align_bytes=64) for a in range(PASSES)]
         slot_codes = [work.tile([P, S], U32, name=f"slot_codes{a}", align_bytes=64) for a in range(PASSES)]
         slot_scales = [work.tile([P, S], U8, name=f"slot_scales{a}", align_bytes=64) for a in range(PASSES)]
@@ -77,17 +76,20 @@ def tile_moe_shr_lin_none_kernel(tc, xT, w_words, w_scales, gate, offs, pos1, po
         def cast(engine_copy, a, u, t0, t1):
             engine_copy(out=pairs[:, block[a, u], t0:t1, :], in_=raw[a, u][:, :, t0:t1].rearrange("p j t -> p t j"))
 
-        def gather(a, u, lo, hi):
+        def planes_tile(tag, n):
+            return work.tile([P, 2, n, 2], BF16, name="planes", tag=tag, align_bytes=64)
+
+        def gather(planes, base, a, u, lo, hi):
             start = block[a, u] * T
             stop = start + T if a == 0 else start + 2 * T
             window = pair_words[:, start:stop]
-            dst = planes[a][:, u, lo:hi, :].rearrange("p s d -> p (s d)").bitcast(U32)
+            dst = planes[:, u, lo - base : hi - base, :].rearrange("p s d -> p (s d)").bitcast(U32)
             nc.vector.tensor_copy(dst, window.indirect(offs_t[:, lo // 16 : hi // 16]))
 
-        def interleave_slots(copy, dtype, a, lo, hi):
-            src = planes[a][:].rearrange("p u s d -> p (u s d)").bitcast(dtype).rearrange("p (u s) -> p s u", u=2)
+        def interleave_slots(copy, dtype, planes, a, lo, hi):
+            src = planes[:].rearrange("p u s d -> p (u s d)").bitcast(dtype).rearrange("p (u s) -> p s u", u=2)
             dst = slots[a][:].rearrange("p s d -> p (s d)").bitcast(dtype).rearrange("p (s u) -> p s u", u=2)
-            copy(out=dst[:, lo:hi, :], in_=src[:, lo:hi, :])
+            copy(out=dst[:, lo:hi, :], in_=src)
 
         def quantize_slots(a, lo, hi):
             nc.vector.quantize_mx(
@@ -135,35 +137,43 @@ def tile_moe_shr_lin_none_kernel(tc, xT, w_words, w_scales, gate, offs, pos1, po
         cast(nc.scalar.copy, 0, 1, 0, T)
         cast(nc.scalar.copy, 1, 0, 0, T)
         cast(nc.scalar.copy, 1, 1, 0, T)
-        for lo, hi in ((0, 448), (448, 864), (864, S)):
-            gather(0, 0, lo, hi)
-        for half in (0, 640):
-            gather(0, 1, half, half + 320)
-            gather(0, 1, half + 320, half + 640)
-            interleave_slots(nc.scalar.copy, U32, 0, half, half + 640)
+        halves = [planes_tile("planes_a", 640), planes_tile("planes_b", 640)]
+        for lo, hi in ((0, 320), (320, 640)):
+            gather(halves[0], 0, 0, 0, lo, hi)
+        for lo, hi in ((640, 960), (960, S)):
+            gather(halves[1], 640, 0, 0, lo, hi)
+        for lo, hi in ((0, 320), (320, 640)):
+            gather(halves[0], 0, 0, 1, lo, hi)
+        interleave_slots(nc.scalar.copy, U32, halves[0], 0, 0, 640)
+        for lo, hi in ((640, 960), (960, S)):
+            gather(halves[1], 640, 0, 1, lo, hi)
+        interleave_slots(nc.scalar.copy, U32, halves[1], 0, 640, S)
+        part0 = planes_tile("planes_c", 512)
         for u in range(2):
-            gather(1, u, 0, 512)
-        interleave_slots(nc.scalar.copy, U32, 1, 0, 512)
+            gather(part0, 0, 1, u, 0, 512)
+        interleave_slots(nc.scalar.copy, U32, part0, 1, 0, 512)
         quantize_slots(0, 0, 1024)
         quantize_slots(0, 1024, S)
+        part1 = planes_tile("planes_b", 512)
         for u in range(2):
-            gather(1, u, 512, 1024)
-        interleave_slots(nc.scalar.copy, U32, 1, 512, 1024)
+            gather(part1, 512, 1, u, 512, 1024)
+        interleave_slots(nc.scalar.copy, U32, part1, 1, 512, 1024)
         quantize_slots(1, 0, 512)
         for m in range(M):
             experts(m, 0, 4)
+        part2 = planes_tile("planes_c", 256)
         for u in range(2):
-            gather(1, u, 1024, S)
+            gather(part2, 1024, 1, u, 1024, S)
         quantize_slots(1, 512, 1024)
-        interleave_slots(nc.vector.tensor_copy, I32, 1, 1024, S)
+        interleave_slots(nc.vector.tensor_copy, I32, part2, 1, 1024, S)
         interleave_toks(0)
         interleave_toks(1)
+        quantize_toks(1024, PASSES * T)
         quantize_slots(1, 1024, S)
         for m in range(M):
             experts(m, 4, 8)
             experts(m, 8, 10)
         quantize_toks(0, 1024)
-        quantize_toks(1024, PASSES * T)
 
         ys = [psum.tile([P, 512], F32, name=f"ys{m}") for m in range(M)]
         shared = [work.tile([P, T], F32, name=f"shared{m}") for m in range(M)]

@@ -16,6 +16,7 @@ FP8X4 = mybir.dt.float8_e4m3fn_x4
 FP4X4 = mybir.dt.float4_e2m1fn_x4
 MULT = mybir.AluOpType.mult
 ADD = mybir.AluOpType.add
+COPY = mybir.ActivationFunctionType.Copy
 
 P = 128
 PASSES = 2
@@ -33,17 +34,18 @@ def tile_moe_shr_lin_none_kernel(tc, xT, w_words, w_scales, gate, offs, pos1, po
         pos1_t = keep.tile([P, T // 16], U16, name="pos1_t")
         pos2_t = keep.tile([P, T // 16], U16, name="pos2_t")
 
-        raw = {}
-        for a in range(PASSES):
-            for u in range(2):
-                raw[a, u] = work.tile([P, 2, T], F32, name=f"raw{a}{u}")
-        x_view = xT.rearrange("(a p u j) t -> a u p j t", a=PASSES, p=P, u=2, j=2)
-        nc.sync.dma_start(raw[0, 0][:, :, :320], x_view[0, 0][:, :, :320])
-        nc.sync.dma_start(raw[0, 0][:, :, 320:], x_view[0, 0][:, :, 320:])
+        raw = [work.tile([P, 4, T], F32, name=f"raw{a}") for a in range(PASSES)]
+        x_view = xT.rearrange("(a p j) t -> a p j t", a=PASSES, p=P, j=4)
+
+        def load_x(a, u, t0, t1):
+            nc.sync.dma_start(raw[a][:, 2 * u : 2 * u + 2, t0:t1], x_view[a][:, 2 * u : 2 * u + 2, t0:t1])
+
+        load_x(0, 0, 0, 320)
+        load_x(0, 0, 320, T)
         nc.sync.dma_start(offs_t[:], offs)
-        nc.sync.dma_start(raw[0, 1][:], x_view[0, 1])
-        nc.sync.dma_start(raw[1, 0][:], x_view[1, 0])
-        nc.sync.dma_start(raw[1, 1][:], x_view[1, 1])
+        load_x(0, 1, 0, T)
+        load_x(1, 0, 0, T)
+        load_x(1, 1, 0, T)
 
         ws = work.tile([P, (E + 1) * PASSES, N], U8, name="ws", align_bytes=64)
         nc.vector.memset(ws[:].rearrange("p e n -> p (e n)").bitcast(I32), 0)
@@ -65,6 +67,7 @@ def tile_moe_shr_lin_none_kernel(tc, xT, w_words, w_scales, gate, offs, pos1, po
 
         pairs = work.tile([P, 2 * PASSES, T, 2], BF16, name="pairs", align_bytes=64)
         pair_words = pairs[:].rearrange("p b t d -> p (b t d)").bitcast(U32)
+        last_rows = work.tile([P, 2, T], BF16, name="last_rows", align_bytes=64)
         block = {(1, 0): 0, (1, 1): 1, (0, 0): 2, (0, 1): 3}
         slots = [work.tile([P, S, 4], BF16, name=f"slots{a}", align_bytes=64) for a in range(PASSES)]
         slot_codes = [work.tile([P, S], U32, name=f"slot_codes{a}", align_bytes=64) for a in range(PASSES)]
@@ -74,7 +77,10 @@ def tile_moe_shr_lin_none_kernel(tc, xT, w_words, w_scales, gate, offs, pos1, po
         tok_scales = work.tile([P, PASSES * T], U8, name="tok_scales", align_bytes=64)
 
         def cast(engine_copy, a, u, t0, t1):
-            engine_copy(out=pairs[:, block[a, u], t0:t1, :], in_=raw[a, u][:, :, t0:t1].rearrange("p j t -> p t j"))
+            engine_copy(out=pairs[:, block[a, u], t0:t1, :], in_=raw[a][:, 2 * u : 2 * u + 2, t0:t1].rearrange("p j t -> p t j"))
+
+        def round_on_gpsimd(out, in_):
+            nc.gpsimd.tensor_scalar(out, in_, 1.0, 0.0, MULT, ADD)
 
         def planes_tile(tag, n):
             return work.tile([P, 2, n, 2], BF16, name="planes", tag=tag, align_bytes=64)
@@ -105,10 +111,18 @@ def tile_moe_shr_lin_none_kernel(tc, xT, w_words, w_scales, gate, offs, pos1, po
                 in_=toks[:, lo:hi, :].rearrange("p s d -> p (s d)"),
             )
 
-        def interleave_toks(a):
-            src = pair_words[:, block[a, 0] * T : (block[a, 0] + 2) * T].rearrange("p (u t) -> p t u", u=2)
-            dst = toks[:, a * T : (a + 1) * T, :].rearrange("p t d -> p (t d)").bitcast(U32).rearrange("p (t u) -> p t u", u=2)
-            nc.scalar.copy(out=dst, in_=src)
+        def round_toks(a):
+            for t0 in (0, 320):
+                dst = toks[:, a * T + t0 : a * T + t0 + 320, :]
+                round_on_gpsimd(dst, raw[a][:, :, t0 : t0 + 320].rearrange("p j t -> p t j"))
+
+        def gather_on_scalar(planes, base, e):
+            for d in range(2):
+                nc.scalar.activation(
+                    planes[:, 1, e * C - base : (e + 1) * C - base, d],
+                    last_rows[:, d, :].indirect(offs_t[:, e * C // 16 : (e + 1) * C // 16]),
+                    COPY,
+                )
 
         def matmul(dst, e, a, m, codes, scales):
             nc.tensor.matmul_mx(
@@ -133,10 +147,14 @@ def tile_moe_shr_lin_none_kernel(tc, xT, w_words, w_scales, gate, offs, pos1, po
 
         for half in (0, 320):
             cast(nc.vector.tensor_copy, 0, 0, half, half + 208)
-            cast(nc.scalar.copy, 0, 0, half + 208, half + 320)
+            cast(lambda out, in_: nc.scalar.activation(out, in_, COPY), 0, 0, half + 208, half + 320)
         cast(nc.scalar.copy, 0, 1, 0, T)
         cast(nc.scalar.copy, 1, 0, 0, T)
         cast(nc.scalar.copy, 1, 1, 0, T)
+        round_toks(0)
+        for d in range(2):
+            round_on_gpsimd(last_rows[:, d, :], raw[1][:, 2 + d, :])
+        round_toks(1)
         halves = [planes_tile("planes_a", 640), planes_tile("planes_b", 640)]
         for lo, hi in ((0, 320), (320, 640)):
             gather(halves[0], 0, 0, 0, lo, hi)
@@ -155,8 +173,9 @@ def tile_moe_shr_lin_none_kernel(tc, xT, w_words, w_scales, gate, offs, pos1, po
         quantize_slots(0, 0, 1024)
         quantize_slots(0, 1024, S)
         part1 = planes_tile("planes_b", 512)
-        for u in range(2):
-            gather(part1, 512, 1, u, 512, 1024)
+        gather(part1, 512, 1, 0, 512, 1024)
+        for e in range(4, 8):
+            gather_on_scalar(part1, 512, e)
         interleave_slots(nc.scalar.copy, U32, part1, 1, 512, 1024)
         quantize_slots(1, 0, 512)
         for m in range(M):
@@ -166,14 +185,12 @@ def tile_moe_shr_lin_none_kernel(tc, xT, w_words, w_scales, gate, offs, pos1, po
             gather(part2, 1024, 1, u, 1024, S)
         quantize_slots(1, 512, 1024)
         interleave_slots(nc.vector.tensor_copy, I32, part2, 1, 1024, S)
-        interleave_toks(0)
-        interleave_toks(1)
-        quantize_toks(1024, PASSES * T)
         quantize_slots(1, 1024, S)
         for m in range(M):
             experts(m, 4, 8)
             experts(m, 8, 10)
         quantize_toks(0, 1024)
+        quantize_toks(1024, PASSES * T)
 
         ys = [psum.tile([P, 512], F32, name=f"ys{m}") for m in range(M)]
         shared = [work.tile([P, T], F32, name=f"shared{m}") for m in range(M)]

from contextlib import ExitStack

import concourse.mybir as mybir

K, T, E, C, N = 1024, 640, 10, 128, 384
S = E * C
FLOPS = 2 * K * N * (S + T)

F32 = mybir.dt.float32
BF16 = mybir.dt.bfloat16
U32 = mybir.dt.uint32
I32 = mybir.dt.int32
U16 = mybir.dt.uint16
U8 = mybir.dt.uint8
FP8X4 = mybir.dt.float8_e4m3fn_x4
FP4X4 = mybir.dt.float4_e2m1fn_x4
MULT = mybir.AluOpType.mult
ADD = mybir.AluOpType.add
COPY = mybir.ActivationFunctionType.Copy

P = 128
PASSES = 2
M = N // P


def tile_moe_shr_lin_none_kernel(tc, xT, w_words, w_scales, gate, offs, pos1, pos2, out):
    nc = tc.nc
    with ExitStack() as ctx:
        keep = ctx.enter_context(tc.tile_pool(name="keep", bufs=1))
        work = ctx.enter_context(tc.tile_pool(name="work", bufs=1))
        psum = ctx.enter_context(tc.psum_pool(name="psum", bufs=1))

        offs_t = keep.tile([P, S // 16], U16, name="offs_t")
        pos1_t = keep.tile([P, T // 16], U16, name="pos1_t")
        pos2_t = keep.tile([P, T // 16], U16, name="pos2_t")

        raw = [work.tile([P, 4, T], F32, name=f"raw{a}") for a in range(PASSES)]
        x_view = xT.rearrange("(a p j) t -> a p j t", a=PASSES, p=P, j=4)

        def load_x(a, u, t0, t1):
            nc.sync.dma_start(raw[a][:, 2 * u : 2 * u + 2, t0:t1], x_view[a][:, 2 * u : 2 * u + 2, t0:t1])

        load_x(0, 0, 0, 320)
        load_x(0, 0, 320, T)
        nc.sync.dma_start(offs_t[:], offs)
        load_x(0, 1, 0, T)
        load_x(1, 0, 0, T)
        load_x(1, 1, 0, T)

        ws = work.tile([P, (E + 1) * PASSES, N], U8, name="ws", align_bytes=64)
        nc.vector.memset(ws[:].rearrange("p e n -> p (e n)").bitcast(I32), 0)
        s_view = w_scales.rearrange("e a q n -> q (e a) n").bitcast(I32)
        for q in range(4):
            nc.sync.dma_start(ws[32 * q : 32 * q + 4].bitcast(I32), s_view[4 * q : 4 * q + 4])

        ww = work.tile([P, (E + 1) * PASSES, 2 * N], U8, name="ww", align_bytes=64)
        w_view = w_words.rearrange("e a p b -> p (e a) b").bitcast(I32)
        for e0, e1 in ((0, 4), (4, 8), (8, 11)):
            nc.sync.dma_start(ww[:, PASSES * e0 : PASSES * e1, :].bitcast(I32), w_view[:, PASSES * e0 : PASSES * e1, :])
        nc.sync.dma_start(pos1_t[:], pos1)
        nc.sync.dma_start(pos2_t[:], pos2)
        gates = []
        for m in range(M):
            g = work.tile([P, 2, T], F32, name=f"gate{m}")
            nc.sync.dma_start(g[:], gate[:, m * P : (m + 1) * P, :].rearrange("g p t -> p g t"))
            gates.append(g)

        pairs = work.tile([P, 2 * PASSES, T, 2], BF16, name="pairs", align_bytes=64)
        pair_words = pairs[:].rearrange("p b t d -> p (b t d)").bitcast(U32)
        last_rows = work.tile([P, 2, T], BF16, name="last_rows", align_bytes=64)
        block = {(1, 0): 0, (1, 1): 1, (0, 0): 2, (0, 1): 3}
        slots = [work.tile([P, S, 4], BF16, name=f"slots{a}", align_bytes=64) for a in range(PASSES)]
        slot_codes = [work.tile([P, S], U32, name=f"slot_codes{a}", align_bytes=64) for a in range(PASSES)]
        slot_scales = [work.tile([P, S], U8, name=f"slot_scales{a}", align_bytes=64) for a in range(PASSES)]
        toks = work.tile([P, PASSES * T, 4], BF16, name="toks", align_bytes=64)
        tok_codes = work.tile([P, PASSES * T], U32, name="tok_codes", align_bytes=64)
        tok_scales = work.tile([P, PASSES * T], U8, name="tok_scales", align_bytes=64)

        def cast(engine_copy, a, u, t0, t1):
            engine_copy(out=pairs[:, block[a, u], t0:t1, :], in_=raw[a][:, 2 * u : 2 * u + 2, t0:t1].rearrange("p j t -> p t j"))

        def round_on_gpsimd(out, in_):
            nc.gpsimd.tensor_scalar(out, in_, 1.0, 0.0, MULT, ADD)

        def planes_tile(tag, n):
            return work.tile([P, 2, n, 2], BF16, name="planes", tag=tag, align_bytes=64)

        def gather(planes, base, a, u, lo, hi):
            start = block[a, u] * T
            stop = start + T if a == 0 else start + 2 * T
            window = pair_words[:, start:stop]
            dst = planes[:, u, lo - base : hi - base, :].rearrange("p s d -> p (s d)").bitcast(U32)
            nc.vector.tensor_copy(dst, window.indirect(offs_t[:, lo // 16 : hi // 16]))

        def interleave_slots(copy, dtype, planes, a, lo, hi):
            src = planes[:].rearrange("p u s d -> p (u s d)").bitcast(dtype).rearrange("p (u s) -> p s u", u=2)
            dst = slots[a][:].rearrange("p s d -> p (s d)").bitcast(dtype).rearrange("p (s u) -> p s u", u=2)
            copy(out=dst[:, lo:hi, :], in_=src)

        def quantize_slots(a, lo, hi):
            nc.vector.quantize_mx(
                out=slot_codes[a][:, lo:hi].bitcast(FP8X4),
                scales=slot_scales[a][:, lo:hi],
                in_=slots[a][:, lo:hi, :].rearrange("p s d -> p (s d)"),
            )

        def quantize_toks(lo, hi):
            nc.vector.quantize_mx(
                out=tok_codes[:, lo:hi].bitcast(FP8X4),
                scales=tok_scales[:, lo:hi],
                in_=toks[:, lo:hi, :].rearrange("p s d -> p (s d)"),
            )

        def round_toks(a):
            for t0 in (0, 320):
                dst = toks[:, a * T + t0 : a * T + t0 + 320, :]
                round_on_gpsimd(dst, raw[a][:, :, t0 : t0 + 320].rearrange("p j t -> p t j"))

        def gather_on_scalar(planes, base, e):
            for d in range(2):
                nc.scalar.activation(
                    planes[:, 1, e * C - base : (e + 1) * C - base, d],
                    last_rows[:, d, :].indirect(offs_t[:, e * C // 16 : (e + 1) * C // 16]),
                    COPY,
                )

        def matmul(dst, e, a, m, codes, scales):
            nc.tensor.matmul_mx(
                out=dst,
                lhsT=ww[:, PASSES * e + a, 2 * m * P : 2 * (m + 1) * P].bitcast(FP4X4),
                lhsT_scale=ws[:, PASSES * e + a, m * P : (m + 1) * P],
                rhs=codes.bitcast(FP8X4),
                rhs_scale=scales,
                start=(a == 0),
                stop=(a == PASSES - 1),
            )

        y = [work.tile([P, S], F32, name=f"y{m}") for m in range(M)]

        def experts(m, e0, e1):
            bank = psum.tile([P, 512], F32, name="bank", bufs=4)
            for e in range(e0, e1):
                for a in range(PASSES):
                    cols = slice(e * C, (e + 1) * C)
                    matmul(bank[:, (e - e0) * C : (e - e0 + 1) * C], e, a, m, slot_codes[a][:, cols], slot_scales[a][:, cols])
            nc.scalar.copy(out=y[m][:, e0 * C : e1 * C], in_=bank[:, : (e1 - e0) * C])

        for half in (0, 320):
            cast(nc.vector.tensor_copy, 0, 0, half, half + 208)
            cast(lambda out, in_: nc.scalar.activation(out, in_, COPY), 0, 0, half + 208, half + 320)
        cast(nc.scalar.copy, 0, 1, 0, T)
        cast(nc.scalar.copy, 1, 0, 0, T)
        cast(nc.scalar.copy, 1, 1, 0, T)
        round_toks(0)
        for d in range(2):
            round_on_gpsimd(last_rows[:, d, :], raw[1][:, 2 + d, :])
        round_toks(1)
        halves = [planes_tile("planes_a", 640), planes_tile("planes_b", 640)]
        for lo, hi in ((0, 320), (320, 640)):
            gather(halves[0], 0, 0, 0, lo, hi)
        for lo, hi in ((640, 960), (960, S)):
            gather(halves[1], 640, 0, 0, lo, hi)
        for lo, hi in ((0, 320), (320, 640)):
            gather(halves[0], 0, 0, 1, lo, hi)
        interleave_slots(nc.scalar.copy, U32, halves[0], 0, 0, 640)
        for lo, hi in ((640, 960), (960, S)):
            gather(halves[1], 640, 0, 1, lo, hi)
        interleave_slots(nc.scalar.copy, U32, halves[1], 0, 640, S)
        part0 = planes_tile("planes_c", 512)
        for u in range(2):
            gather(part0, 0, 1, u, 0, 512)
        interleave_slots(nc.scalar.copy, U32, part0, 1, 0, 512)
        quantize_slots(0, 0, 1024)
        quantize_slots(0, 1024, S)
        part1 = planes_tile("planes_b", 512)
        gather(part1, 512, 1, 0, 512, 1024)
        for e in range(4, 8):
            gather_on_scalar(part1, 512, e)
        interleave_slots(nc.scalar.copy, U32, part1, 1, 512, 1024)
        quantize_slots(1, 0, 512)
        for m in range(M):
            experts(m, 0, 4)
        part2 = planes_tile("planes_c", 256)
        for u in range(2):
            gather(part2, 1024, 1, u, 1024, S)
        quantize_slots(1, 512, 1024)
        interleave_slots(nc.vector.tensor_copy, I32, part2, 1, 1024, S)
        quantize_slots(1, 1024, S)
        for m in range(M):
            experts(m, 4, 8)
            experts(m, 8, 10)
        quantize_toks(0, 1024)
        quantize_toks(1024, PASSES * T)

        ys = [psum.tile([P, 512], F32, name=f"ys{m}") for m in range(M)]
        shared = [work.tile([P, T], F32, name=f"shared{m}") for m in range(M)]
        ys_tail = psum.tile([P, M, P], F32, name="ys_tail")
        for m in range(M):
            for dst, lo, hi in ((ys[m][:], 0, 512), (ys_tail[:, m, :], 512, T)):
                for a in range(PASSES):
                    matmul(dst, E, a, m, tok_codes[:, a * T + lo : a * T + hi], tok_scales[:, a * T + lo : a * T + hi])
            nc.scalar.copy(out=shared[m][:, :512], in_=ys[m][:])
            nc.scalar.copy(out=shared[m][:, 512:], in_=ys_tail[:, m, :])

        first = [work.tile([P, T], F32, name=f"first{m}") for m in range(M)]
        second = [work.tile([P, T], F32, name=f"second{m}") for m in range(M)]
        both = [work.tile([P, T], F32, name=f"both{m}") for m in range(M)]
        res = [work.tile([P, T], F32, name=f"res{m}") for m in range(M)]

        def pick1(m):
            nc.vector.tensor_tensor(first[m][:], y[m][:].indirect(pos1_t[:]), gates[m][:, 0, :], MULT)

        def pick2(m, lo, hi):
            nc.vector.tensor_tensor(second[m][:, lo:hi], y[m][:].indirect(pos2_t[:, lo // 16 : hi // 16]), gates[m][:, 1, lo:hi], MULT)

        def add(m, lo, hi):
            nc.vector.tensor_tensor(both[m][:, lo:hi], first[m][:, lo:hi], second[m][:, lo:hi], ADD)

        def finish(m, lo, hi):
            nc.vector.tensor_tensor(res[m][:, lo:hi], shared[m][:, lo:hi], both[m][:, lo:hi], ADD)
            nc.sync.dma_start(out[m * P : (m + 1) * P, lo:hi], res[m][:, lo:hi])

        pick1(0)
        pick2(0, 0, T)
        pick1(1)
        add(0, 0, T)
        pick2(1, 0, T)
        finish(0, 0, T)
        pick1(2)
        add(1, 0, T)
        pick2(2, 0, 448)
        finish(1, 0, T)
        pick2(2, 448, T)
        add(2, 0, 448)
        add(2, 448, T)
        finish(2, 0, 448)
        finish(2, 448, T)
